import numpy as np
import ml_dtypes


def mxq(x, axis, fmt="e4m3"):
    dtype, down = {"e4m3": (ml_dtypes.float8_e4m3fn, 7), "e5m2": (ml_dtypes.float8_e5m2, 14)}[fmt]
    v = np.moveaxis(np.asarray(x, np.float32).astype(ml_dtypes.bfloat16).astype(np.float64), axis, -1)
    blocks = v.reshape(v.shape[:-1] + (-1, 32))
    amax = np.abs(blocks).max(-1, keepdims=True)
    byte = np.maximum(np.where(amax > 0, np.frexp(amax)[1] - 1 + 127, 0) - down, 1)
    scale = np.exp2(byte - 127.0)
    codes = (blocks / scale).astype(np.float32).astype(dtype).astype(np.float64)
    return np.moveaxis((codes * scale).reshape(v.shape), -1, axis)


WIDE = False


def mx_kscale(k):
    if not WIDE:
        return np.ones(k)
    levels = np.array([18, -18])
    if k % 512:
        return np.exp2(np.random.permutation(np.resize(levels, k // 32))).repeat(32)
    a = np.empty((k // 512, 16))
    for p in range(k // 512):
        a[p, :8] = np.random.permutation(np.resize(levels, 8))
        for g in range(8):
            far = levels[np.abs(levels - a[p, g]) >= 10]
            a[p, g + 8] = far[np.random.randint(len(far))]
    return np.exp2(a.ravel()).repeat(32)


def f64(x):
    return np.asarray(x).astype(np.float64)


def striped(idx):
    return np.tile(np.asarray(idx).reshape(-1, 16).T, (8, 1)).astype(np.uint16)


def unstriped(offs):
    return offs[:16].T.reshape(-1).astype(np.int64)


B, N, T, D, R, TU = 2, 512, 2048, 512, 512, 2048


def setup_inputs():
    n = np.random.standard_normal
    idx = np.random.permutation(T)[:B * N]
    uidx = np.random.permutation(TU)[:B * R]
    s = mx_kscale(D)[:, None]
    z = np.ones(TU)
    z[uidx] = mx_kscale(B * R)
    u = np.ones(T)
    u[idx] = mx_kscale(B * N)
    r = np.random.uniform(0.5, 2.0, T) * u
    ur = np.random.uniform(0.5, 2.0, TU) * z
    return {
        "uT": (n((D, TU)) * s / ur).astype(np.float32),
        "vT": (n((D, T)) * (1.00 / np.sqrt(D)) / s / r).astype(np.float32),
        "y": n((B, R, N)).astype(np.float32),
        "us": ur[uidx].reshape(B, R, 1).astype(np.float32),
        "ts": np.tile(r, (128, 1)).astype(np.float32),
        "offs": striped(idx),
        "uoffs": striped(uidx),
    }


def reference(uT, vT, y, us, ts, offs, uoffs):
    idx = unstriped(offs)
    pick = lambda x: x[:, idx].reshape(x.shape[0], B, N).transpose(1, 0, 2)
    uidx = unstriped(uoffs)
    w = pick(f64(vT))
    x = f64(uT)[:, uidx].reshape(D, B, R).transpose(1, 0, 2)
    a = mxq(x, 1, "e4m3").transpose(0, 2, 1) @ mxq(w, 1, "e4m3")
    sc = f64(us) * pick(f64(ts))[:, :1, :]
    a = a * sc
    g = np.tanh(a - f64(y))
    h = sc * g
    dv = mxq(x, 2, "e4m3") @ mxq(h, 1, "e5m2")
    gv = np.zeros((D, T))
    gv[:, idx] = dv.transpose(1, 0, 2).reshape(D, B * N)
    du = mxq(w, 2, "e4m3") @ mxq(h, 2, "e5m2").transpose(0, 2, 1)
    gu = np.zeros((D, TU))
    gu[:, uidx] = du.transpose(1, 0, 2).reshape(D, B * R)
    return gv, gu

@@ -1,0 +1,201 @@
+from contextlib import ExitStack
+
+import concourse.mybir as mybir
+from concourse.masks import make_identity
+
+B, N, T, D, R, TU = 2, 512, 2048, 512, 512, 2048
+FLOPS = 3 * 2 * B * R * N * D
+
+F32 = mybir.dt.float32
+BF16 = mybir.dt.bfloat16
+U32 = mybir.dt.uint32
+U16 = mybir.dt.uint16
+U8 = mybir.dt.uint8
+E4M3 = mybir.dt.float8_e4m3fn_x4
+E5M2 = mybir.dt.float8_e5m2_x4
+COPY = mybir.ActivationFunctionType.Copy
+TANH = mybir.ActivationFunctionType.Tanh
+MULT = mybir.AluOpType.mult
+
+P = 128
+PACK = 4
+K = P * PACK
+LIST_COLS = K // 16
+
+
+def tile_attend_gmf_lch_vu_kernel(tc, uT, vT, y, us, ts, offs, uoffs, out_0, out_1):
+    nc = tc.nc
+    with ExitStack() as ctx:
+        held = ctx.enter_context(tc.tile_pool(name="held", bufs=1))
+        planes = ctx.enter_context(tc.tile_pool(name="planes", bufs=6))
+        packed = ctx.enter_context(tc.tile_pool(name="packed", bufs=4))
+        ring = ctx.enter_context(tc.tile_pool(name="ring", bufs=3))
+        staged = ctx.enter_context(tc.tile_pool(name="staged", bufs=10))
+        psum = ctx.enter_context(tc.psum_pool(name="psum", bufs=2))
+
+        u_list = held.tile([P, B * LIST_COLS], U16, name="u_list")
+        v_list = held.tile([P, B * LIST_COLS], U16, name="v_list")
+
+        def entries(a_list, b):
+            return a_list[:, b * LIST_COLS : (b + 1) * LIST_COLS]
+
+        def load_plane(table, t):
+            plane = planes.tile([P, T], F32, name="plane")
+            nc.sync.dma_start(plane[:], table.rearrange("(p t) c -> p t c", t=PACK)[:, t, :])
+            return plane
+
+        nc.sync.dma_start(u_list[:], uoffs)
+        u_planes = [load_plane(uT, 0)]
+        nc.sync.dma_start(v_list[:], offs)
+        u_planes.extend(load_plane(uT, t) for t in range(1, PACK))
+
+        ident_bf = held.tile([P, P], BF16, name="ident_bf")
+        ident_f32 = held.tile([P, P], F32, name="ident_f32")
+        make_identity(nc, ident_bf[:])
+        make_identity(nc, ident_f32[:])
+
+        windows = {}
+        for n, (t, o) in enumerate((t, o) for t in range(PACK) for o in (1, 0)):
+            windows[o, t] = held.tile([P, T], F32, name="window%d%d" % (o, t))
+            (nc.vector if n < 3 else nc.gpsimd).memset(windows[o, t][:], 0.0)
+
+        x_cols = [held.tile([P, PACK, K], BF16, name="x_cols%d" % b) for b in range(B)]
+        w_cols = [held.tile([P, PACK, K], BF16, name="w_cols%d" % b) for b in range(B)]
+
+        def gather(cols, t, plane, offsets):
+            nc.vector.tensor_copy(cols[:, t, :].rearrange("p (u m e) -> p m u e", u=2, e=2), plane[:].indirect(offsets))
+
+        def quantize(values, fmt, name):
+            codes = held.tile([P, K], U32, name=name + "_codes", align_bytes=64)
+            scales = held.tile([P, K], U8, name=name + "_scales", align_bytes=64)
+            nc.vector.quantize_mx(out=codes[:].bitcast(fmt), scales=scales[:], in_=values[:].rearrange("p c t -> p (c t)"))
+            return codes, scales, fmt
+
+        def product(stationary, j, moving):
+            acc = psum.tile([P, K], F32, name="acc")
+            cols = slice(j * P, (j + 1) * P)
+            nc.tensor.matmul_mx(
+                out=acc[:],
+                lhsT=stationary[0][:, cols].bitcast(stationary[2]),
+                lhsT_scale=stationary[1][:, cols],
+                rhs=moving[0][:].bitcast(moving[2]),
+                rhs_scale=moving[1][:],
+                start=True,
+                stop=True,
+            )
+            return acc
+
+        def along_d(cols, name):
+            values = packed.tile([P, K, PACK], BF16, name="values", align_bytes=64)
+            for u in range(2):
+                nc.scalar.copy(
+                    values[:, u * 2 * P : (u + 1) * 2 * P, :].rearrange("p (e m) t -> p e m t", e=2),
+                    cols[:, :, u * 2 * P : (u + 1) * 2 * P].rearrange("p t (m e) -> p e m t", e=2),
+                )
+            return quantize(values, E4M3, name)
+
+        def turn(block, fmt, name):
+            values = packed.tile([P, K, PACK], BF16, name="values", align_bytes=64)
+            for half in range(2):
+                turned = psum.tile([P, 2, PACK, P], BF16, name="turned")
+                for e in range(2):
+                    for j in range(PACK):
+                        nc.tensor.transpose(turned[:, e, j, :], block(2 * half + e, j), ident_bf[:])
+                nc.scalar.copy(
+                    values[:, half * 2 * P : (half + 1) * 2 * P, :].rearrange("p (e c) j -> p e c j", e=2),
+                    turned[:].rearrange("p e j c -> p e c j"),
+                )
+            return quantize(values, fmt, name)
+
+        def along_list(cols, name):
+            values = packed.tile([P, K, PACK], BF16, name="values", align_bytes=64)
+            pairs = cols[:].bitcast(F32)
+            value_pairs = values[:].bitcast(F32)
+            for half in range(2):
+                turned = psum.tile([P, 2, 2, P], F32, name="turned")
+                for e in range(2):
+                    for u in range(2):
+                        nc.tensor.transpose(turned[:, e, u, :], pairs[:, 2 * half + e, u * P : (u + 1) * P], ident_f32[:])
+                nc.scalar.copy(
+                    value_pairs[:, half * 2 * P : (half + 1) * 2 * P, :].rearrange("p (e c) u -> p e c u", e=2),
+                    turned[:].rearrange("p e u c -> p e c u"),
+                )
+            return quantize(values, E4M3, name)
+
+        for t in range(PACK):
+            for b in range(B):
+                gather(x_cols[b], t, u_planes[t], entries(u_list, b))
+
+        v_planes = [load_plane(vT, t) for t in range(PACK)]
+        ts_all = planes.tile([P, T], F32, name="plane")
+        nc.sync.dma_start(ts_all[:], ts)
+        us_rows = held.tile([P, B, PACK], F32, name="us_rows")
+        nc.sync.dma_start(us_rows[:], us.rearrange("b (p t) o -> p b (t o)", t=PACK))
+        y_rows = []
+        for b in range(B):
+            y_b = planes.tile([P, PACK, N], F32, name="plane")
+            nc.sync.dma_start(y_b[:], y[b].rearrange("(p t) i -> p t i", t=PACK))
+            y_rows.append(y_b)
+        minus_us = held.tile([P, B, PACK], F32, name="minus_us")
+        nc.vector.tensor_scalar_mul(minus_us[:], us_rows[:], -1.0)
+
+        def scales_of(b):
+            ts_slots = held.tile([P, N], F32, name="ts_slots%d" % b)
+            nc.vector.tensor_copy(ts_slots[:], ts_all[:].indirect(entries(v_list, b)))
+            minus_sc = held.tile([P, PACK, N], F32, name="minus_sc%d" % b)
+            for t in range(PACK):
+                nc.scalar.activation(
+                    minus_sc[:, t, :].rearrange("p (j m) -> p m j", j=PACK),
+                    ts_slots[:].rearrange("p (m j) -> p m j", j=PACK),
+                    COPY,
+                    scale=minus_us[:, b, t : t + 1],
+                )
+            return minus_sc
+
+        def make_h(b, x_d, w_d, minus_sc):
+            values = packed.tile([P, K, PACK], BF16, name="values", align_bytes=64)
+            for t in range(PACK):
+                gap = psum.tile([P, PACK, P], F32, name="gap")
+                for j in range(PACK):
+                    nc.tensor.matmul(gap[:, j, :], lhsT=y_rows[b][:, t, j:N:PACK], rhs=ident_f32[:], start=(j == 0), stop=False, is_transpose=True)
+                a = product(x_d, t, w_d)
+                minus_a = ring.tile([P, N], F32, name="minus_a")
+                nc.vector.tensor_tensor(minus_a[:], a[:], minus_sc[:, t, :], MULT)
+                for j in range(PACK):
+                    nc.tensor.matmul(gap[:, j, :], lhsT=minus_a[:, j * P : (j + 1) * P], rhs=ident_f32[:], start=False, stop=(j == PACK - 1), is_transpose=True)
+                minus_g = ring.tile([P, P, PACK], F32, name="minus_g")
+                nc.scalar.activation(minus_g[:], gap[:].rearrange("p j c -> p c j"), TANH)
+                sc_turned = psum.tile([P, PACK, P], F32, name="sc_turned")
+                for j in range(PACK):
+                    nc.tensor.transpose(sc_turned[:, j, :], minus_sc[:, t, j * P : (j + 1) * P], ident_f32[:])
+                nc.vector.tensor_tensor(values[:, t * P : (t + 1) * P, :], minus_g[:], sc_turned[:].rearrange("p j c -> p c j"), MULT)
+            return values
+
+        def finish(o, t, b, stationary, moving):
+            acc = product(stationary, t, moving)
+            result = staged.tile([P, P, PACK], F32, name="result")
+            nc.scalar.copy(result[:], acc[:].rearrange("p (j m) -> p m j", j=PACK))
+            a_list = (v_list, u_list)[o]
+            nc.vector.tensor_copy(windows[o, t][:].indirect(entries(a_list, b)), result[:].rearrange("p m j -> p (m j)"))
+            if b == B - 1:
+                nc.sync.dma_start((out_0, out_1)[o].rearrange("(p t) c -> p t c", t=PACK)[:, t, :], windows[o, t][:])
+
+        x_d, x_r, w_d, minus_sc = {}, {}, {}, {}
+        for b in range(B):
+            x_d[b] = along_d(x_cols[b], "x_d%d" % b)
+            for t in range(PACK):
+                gather(w_cols[b], t, v_planes[t], entries(v_list, b))
+            x_r[b] = along_list(x_cols[b], "x_r%d" % b)
+            w_d[b] = along_d(w_cols[b], "w_d%d" % b)
+            minus_sc[b] = scales_of(b)
+
+        h_i, h_r, w_i = {}, {}, {}
+        for b in range(B):
+            h_values = make_h(b, x_d[b], w_d[b], minus_sc[b])
+            h_i[b] = quantize(h_values, E5M2, "h_i%d" % b)
+            w_i[b] = along_list(w_cols[b], "w_i%d" % b)
+            h_r[b] = turn(lambda c, j: h_values[:, j * P : (j + 1) * P, c], E5M2, "h_r%d" % b)
+        for b in range(B):
+            for t in range(PACK):
+                finish(1, t, b, w_i[b], h_i[b])
+                finish(0, t, b, x_r[b], h_r[b])

@@ -20,6 +20,7 @@ MULT = mybir.AluOpType.mult
 P = 128
 PACK = 4
 K = P * PACK
+HALF = K // 2
 LIST_COLS = K // 16
 
 
@@ -27,11 +28,9 @@ def tile_attend_gmf_lch_vu_kernel(tc, uT, vT, y, us, ts, offs, uoffs, out_0, out
     nc = tc.nc
     with ExitStack() as ctx:
         held = ctx.enter_context(tc.tile_pool(name="held", bufs=1))
-        planes = ctx.enter_context(tc.tile_pool(name="planes", bufs=6))
-        packed = ctx.enter_context(tc.tile_pool(name="packed", bufs=4))
-        ring = ctx.enter_context(tc.tile_pool(name="ring", bufs=3))
-        staged = ctx.enter_context(tc.tile_pool(name="staged", bufs=10))
-        psum = ctx.enter_context(tc.psum_pool(name="psum", bufs=2))
+        ring = ctx.enter_context(tc.tile_pool(name="ring", bufs=4))
+        staged = ctx.enter_context(tc.tile_pool(name="staged", bufs=4))
+        psum = ctx.enter_context(tc.psum_pool(name="psum", bufs=1))
 
         u_list = held.tile([P, B * LIST_COLS], U16, name="u_list")
         v_list = held.tile([P, B * LIST_COLS], U16, name="v_list")
@@ -39,40 +38,62 @@ def tile_attend_gmf_lch_vu_kernel(tc, uT, vT, y, us, ts, offs, uoffs, out_0, out
         def entries(a_list, b):
             return a_list[:, b * LIST_COLS : (b + 1) * LIST_COLS]
 
-        def load_plane(table, t):
-            plane = planes.tile([P, T], F32, name="plane")
+        def load_plane(table, t, room):
+            plane = held.tile([P, T], F32, name="plane", tag="room%d" % room, align_bytes=64)
             nc.sync.dma_start(plane[:], table.rearrange("(p t) c -> p t c", t=PACK)[:, t, :])
             return plane
 
-        nc.sync.dma_start(u_list[:], uoffs)
-        u_planes = [load_plane(uT, 0)]
+        ts_row = held.tile([P, T], F32, name="ts_row", tag="room0")
+        nc.scalar.dma_start(ts_row[0:32, :], ts[0:32, :])
+        nc.vector.memset(ts_row[32:64, :], 0.0)
+        nc.vector.memset(ts_row[64:P, :], 0.0)
+
         nc.sync.dma_start(v_list[:], offs)
-        u_planes.extend(load_plane(uT, t) for t in range(1, PACK))
+        v_planes = [load_plane(vT, t, 1 + t) for t in range(2)]
+        nc.sync.dma_start(u_list[:], uoffs)
+        us_rows = held.tile([P, B, PACK], F32, name="us_rows")
+        nc.sync.dma_start(us_rows[:], us.rearrange("b (p t) o -> p b (t o)", t=PACK))
+        v_planes.extend(load_plane(vT, t, 1 + t) for t in range(2, PACK))
+        u_planes = [load_plane(uT, 0, 5)]
 
         ident_bf = held.tile([P, P], BF16, name="ident_bf")
         ident_f32 = held.tile([P, P], F32, name="ident_f32")
-        make_identity(nc, ident_bf[:])
         make_identity(nc, ident_f32[:])
+        make_identity(nc, ident_bf[:])
 
         windows = {}
         for n, (t, o) in enumerate((t, o) for t in range(PACK) for o in (1, 0)):
             windows[o, t] = held.tile([P, T], F32, name="window%d%d" % (o, t))
-            (nc.vector if n < 3 else nc.gpsimd).memset(windows[o, t][:], 0.0)
+            (nc.vector if n < 1 else nc.gpsimd).memset(windows[o, t][:], 0.0)
 
-        x_cols = [held.tile([P, PACK, K], BF16, name="x_cols%d" % b) for b in range(B)]
+        x_cols = [held.tile([P, PACK, K], BF16, name="x_cols", tag="x_cols%d" % b) for b in range(B)]
         w_cols = [held.tile([P, PACK, K], BF16, name="w_cols%d" % b) for b in range(B)]
 
-        def gather(cols, t, plane, offsets):
-            nc.vector.tensor_copy(cols[:, t, :].rearrange("p (u m e) -> p m u e", u=2, e=2), plane[:].indirect(offsets))
+        def gathered(cols, t):
+            return cols[:, t, :].rearrange("p (u m e) -> p m u e", u=2, e=2)
 
-        def quantize(values, fmt, name):
-            codes = held.tile([P, K], U32, name=name + "_codes", align_bytes=64)
+        def gather_on_vector(cols, t, plane, offsets):
+            nc.vector.tensor_copy(gathered(cols, t), plane[:].indirect(offsets))
+
+        def gather_on_scalar(cols, t, rounded, offsets):
+            nc.scalar.activation(gathered(cols, t), rounded[:].indirect(offsets), COPY)
+
+        def round_plane(plane, name):
+            rounded = held.tile([P, T], BF16, name=name)
+            nc.scalar.activation(rounded[:], plane[:], COPY)
+            return rounded
+
+        def operand(fmt, name, room=None):
+            codes = held.tile([P, K], U32, name=name + "_codes", tag=room or name + "_codes", align_bytes=64)
             scales = held.tile([P, K], U8, name=name + "_scales", align_bytes=64)
-            nc.vector.quantize_mx(out=codes[:].bitcast(fmt), scales=scales[:], in_=values[:].rearrange("p c t -> p (c t)"))
             return codes, scales, fmt
 
-        def product(stationary, j, moving):
-            acc = psum.tile([P, K], F32, name="acc")
+        def quantize(target, values, cols):
+            codes, scales, fmt = target
+            nc.vector.quantize_mx(out=codes[:, cols].bitcast(fmt), scales=scales[:, cols], in_=values[:, cols, :].rearrange("p c t -> p (c t)"))
+
+        def product(stationary, j, moving, bank):
+            acc = psum.tile([P, K], F32, name="acc", tag=bank)
             cols = slice(j * P, (j + 1) * P)
             nc.tensor.matmul_mx(
                 out=acc[:],
@@ -85,117 +106,178 @@ def tile_attend_gmf_lch_vu_kernel(tc, uT, vT, y, us, ts, offs, uoffs, out_0, out
             )
             return acc
 
-        def along_d(cols, name):
-            values = packed.tile([P, K, PACK], BF16, name="values", align_bytes=64)
+        def values_tile(tag):
+            return held.tile([P, K, PACK], BF16, name="values", tag=tag, align_bytes=64)
+
+        def interleave(values, cols, u):
+            half = slice(u * HALF, (u + 1) * HALF)
+            nc.scalar.copy(
+                values[:, half, :].rearrange("p (e m) t -> p e m t", e=2),
+                cols[:, :, half].rearrange("p t (m e) -> p e m t", e=2),
+            )
+            return half
+
+        def along_d(cols, name, tag):
+            values = values_tile(tag)
             for u in range(2):
-                nc.scalar.copy(
-                    values[:, u * 2 * P : (u + 1) * 2 * P, :].rearrange("p (e m) t -> p e m t", e=2),
-                    cols[:, :, u * 2 * P : (u + 1) * 2 * P].rearrange("p t (m e) -> p e m t", e=2),
-                )
-            return quantize(values, E4M3, name)
+                interleave(values, cols, u)
+            target = operand(E4M3, name)
+            quantize(target, values, slice(0, K))
+            return target
 
-        def turn(block, fmt, name):
-            values = packed.tile([P, K, PACK], BF16, name="values", align_bytes=64)
-            for half in range(2):
-                turned = psum.tile([P, 2, PACK, P], BF16, name="turned")
-                for e in range(2):
-                    for j in range(PACK):
-                        nc.tensor.transpose(turned[:, e, j, :], block(2 * half + e, j), ident_bf[:])
-                nc.scalar.copy(
-                    values[:, half * 2 * P : (half + 1) * 2 * P, :].rearrange("p (e c) j -> p e c j", e=2),
-                    turned[:].rearrange("p e j c -> p e c j"),
-                )
-            return quantize(values, fmt, name)
-
-        def along_list(cols, name):
-            values = packed.tile([P, K, PACK], BF16, name="values", align_bytes=64)
+        def along_list(cols, name, tag):
+            values = values_tile(tag)
             pairs = cols[:].bitcast(F32)
             value_pairs = values[:].bitcast(F32)
             for half in range(2):
-                turned = psum.tile([P, 2, 2, P], F32, name="turned")
+                turned = psum.tile([P, 2, 2, P], F32, name="turned", tag="turn%d" % half)
                 for e in range(2):
                     for u in range(2):
                         nc.tensor.transpose(turned[:, e, u, :], pairs[:, 2 * half + e, u * P : (u + 1) * P], ident_f32[:])
                 nc.scalar.copy(
-                    value_pairs[:, half * 2 * P : (half + 1) * 2 * P, :].rearrange("p (e c) u -> p e c u", e=2),
+                    value_pairs[:, half * HALF : (half + 1) * HALF, :].rearrange("p (e c) u -> p e c u", e=2),
                     turned[:].rearrange("p e u c -> p e c u"),
                 )
-            return quantize(values, E4M3, name)
+            target = operand(E4M3, name)
+            quantize(target, values, slice(0, K))
+            return target
 
-        for t in range(PACK):
-            for b in range(B):
-                gather(x_cols[b], t, u_planes[t], entries(u_list, b))
-
-        v_planes = [load_plane(vT, t) for t in range(PACK)]
-        ts_all = planes.tile([P, T], F32, name="plane")
-        nc.sync.dma_start(ts_all[:], ts)
-        us_rows = held.tile([P, B, PACK], F32, name="us_rows")
-        nc.sync.dma_start(us_rows[:], us.rearrange("b (p t) o -> p b (t o)", t=PACK))
-        y_rows = []
-        for b in range(B):
-            y_b = planes.tile([P, PACK, N], F32, name="plane")
-            nc.sync.dma_start(y_b[:], y[b].rearrange("(p t) i -> p t i", t=PACK))
-            y_rows.append(y_b)
-        minus_us = held.tile([P, B, PACK], F32, name="minus_us")
-        nc.vector.tensor_scalar_mul(minus_us[:], us_rows[:], -1.0)
-
-        def scales_of(b):
-            ts_slots = held.tile([P, N], F32, name="ts_slots%d" % b)
-            nc.vector.tensor_copy(ts_slots[:], ts_all[:].indirect(entries(v_list, b)))
-            minus_sc = held.tile([P, PACK, N], F32, name="minus_sc%d" % b)
-            for t in range(PACK):
-                nc.scalar.activation(
-                    minus_sc[:, t, :].rearrange("p (j m) -> p m j", j=PACK),
-                    ts_slots[:].rearrange("p (m j) -> p m j", j=PACK),
-                    COPY,
-                    scale=minus_us[:, b, t : t + 1],
+        def h_along_rows(h_values, name):
+            values = values_tile("values_c")
+            for half in range(2):
+                turned = psum.tile([P, 2, PACK, P], BF16, name="turned", tag="turn%d" % half)
+                for e in range(2):
+                    for t in range(PACK):
+                        nc.tensor.transpose(turned[:, e, t, :], h_values[:, t * P : (t + 1) * P, 2 * half + e], ident_bf[:])
+                nc.scalar.copy(
+                    values[:, half * HALF : (half + 1) * HALF, :].rearrange("p (e m) t -> p e m t", e=2),
+                    turned[:].rearrange("p e t m -> p e m t"),
                 )
-            return minus_sc
+            target = operand(E5M2, name)
+            quantize(target, values, slice(0, K))
+            return target
 
-        def make_h(b, x_d, w_d, minus_sc):
-            values = packed.tile([P, K, PACK], BF16, name="values", align_bytes=64)
+        minus_us = held.tile([P, B, PACK], F32, name="minus_us")
+
+        def ts_column_of(b):
+            ts_slots = held.tile([P, N], F32, name="ts_slots%d" % b)
+            nc.vector.tensor_copy(ts_slots[:], ts_row[:].indirect(entries(v_list, b)))
+            turned = psum.tile([P, PACK, P], F32, name="turned", tag="gap%d" % b)
+            for j in range(PACK):
+                nc.tensor.transpose(turned[:, j, :], ts_slots[:, j:N:PACK], ident_f32[:])
+            ts_column = held.tile([P, PACK], F32, name="ts_column%d" % b)
+            nc.scalar.copy(ts_column[:], turned[:, :, 0])
+            return ts_column
+
+        def spread(columns, bank):
+            rows = psum.tile([P, PACK, P], F32, name="rows", tag=bank)
+            for j in range(PACK):
+                nc.tensor.transpose(rows[:, j, :], columns[:, j : j + 1].to_broadcast([P, P]), ident_f32[:])
+            return rows[:].rearrange("p j m -> p (j m)")
+
+        def scales_of(b, ts_column):
+            ts_spread = held.tile([P, N], F32, name="ts_spread")
+            nc.scalar.copy(ts_spread[:], spread(ts_column, "gap2"))
+            us_spread = spread(minus_us[:, b, :], "gap3")
+            minus_sc = held.tile([P, PACK, R], F32, name="minus_sc")
+            for j in range(PACK):
+                nc.scalar.activation(minus_sc[:, j, :], us_spread, COPY, scale=ts_column[:, j : j + 1])
+            return ts_spread, minus_sc
+
+        def make_h(b, x_d, w_d, scales):
+            ts_spread, minus_sc = scales
+            values = values_tile("values_a")
+            gaps = [psum.tile([P, PACK, P], F32, name="gap", tag="gap%d" % t) for t in range(PACK)]
             for t in range(PACK):
-                gap = psum.tile([P, PACK, P], F32, name="gap")
                 for j in range(PACK):
-                    nc.tensor.matmul(gap[:, j, :], lhsT=y_rows[b][:, t, j:N:PACK], rhs=ident_f32[:], start=(j == 0), stop=False, is_transpose=True)
-                a = product(x_d, t, w_d)
+                    nc.tensor.matmul(gaps[t][:, j, :], lhsT=y_rows[b][:, t, j:N:PACK], rhs=ident_f32[:], start=(j == 0), stop=False, is_transpose=True)
+                a = product(x_d, t, w_d, "acc%d" % (t % 2))
                 minus_a = ring.tile([P, N], F32, name="minus_a")
-                nc.vector.tensor_tensor(minus_a[:], a[:], minus_sc[:, t, :], MULT)
+                nc.vector.scalar_tensor_tensor(minus_a[:], a[:], minus_us[:, b, t : t + 1], ts_spread[:], MULT, MULT)
                 for j in range(PACK):
-                    nc.tensor.matmul(gap[:, j, :], lhsT=minus_a[:, j * P : (j + 1) * P], rhs=ident_f32[:], start=False, stop=(j == PACK - 1), is_transpose=True)
+                    nc.tensor.matmul(gaps[t][:, j, :], lhsT=minus_a[:, j * P : (j + 1) * P], rhs=ident_f32[:], start=False, stop=(j == PACK - 1), is_transpose=True)
                 minus_g = ring.tile([P, P, PACK], F32, name="minus_g")
-                nc.scalar.activation(minus_g[:], gap[:].rearrange("p j c -> p c j"), TANH)
-                sc_turned = psum.tile([P, PACK, P], F32, name="sc_turned")
-                for j in range(PACK):
-                    nc.tensor.transpose(sc_turned[:, j, :], minus_sc[:, t, j * P : (j + 1) * P], ident_f32[:])
-                nc.vector.tensor_tensor(values[:, t * P : (t + 1) * P, :], minus_g[:], sc_turned[:].rearrange("p j c -> p c j"), MULT)
+                nc.scalar.activation(minus_g[:], gaps[t][:].rearrange("p j c -> p c j"), TANH)
+                rows = slice(t * P, (t + 1) * P)
+                nc.vector.tensor_tensor(values[:, rows, :], minus_g[:], minus_sc[:, :, rows].rearrange("p j c -> p c j"), MULT)
             return values
 
-        def finish(o, t, b, stationary, moving):
-            acc = product(stationary, t, moving)
-            result = staged.tile([P, P, PACK], F32, name="result")
+        def result_of(operands, t, bank, room=None):
+            acc = product(operands[0], t, operands[1], bank)
+            if room is None:
+                result = staged.tile([P, P, PACK], F32, name="result")
+            else:
+                result = held.tile([P, P, PACK], F32, name="result", tag=room)
             nc.scalar.copy(result[:], acc[:].rearrange("p (j m) -> p m j", j=PACK))
+            return result
+
+        def scatter(o, t, b, result):
             a_list = (v_list, u_list)[o]
             nc.vector.tensor_copy(windows[o, t][:].indirect(entries(a_list, b)), result[:].rearrange("p m j -> p (m j)"))
             if b == B - 1:
                 nc.sync.dma_start((out_0, out_1)[o].rearrange("(p t) c -> p t c", t=PACK)[:, t, :], windows[o, t][:])
 
-        x_d, x_r, w_d, minus_sc = {}, {}, {}, {}
         for b in range(B):
-            x_d[b] = along_d(x_cols[b], "x_d%d" % b)
-            for t in range(PACK):
-                gather(w_cols[b], t, v_planes[t], entries(v_list, b))
-            x_r[b] = along_list(x_cols[b], "x_r%d" % b)
-            w_d[b] = along_d(w_cols[b], "w_d%d" % b)
-            minus_sc[b] = scales_of(b)
+            gather_on_vector(w_cols[b], 0, v_planes[0], entries(v_list, b))
+        v_rounded = round_plane(v_planes[1], "v_rounded")
+        for b in range(B):
+            gather_on_scalar(w_cols[b], 1, v_rounded, entries(v_list, b))
+        nc.vector.tensor_scalar_mul(minus_us[:], us_rows[:], -1.0)
+        ts_columns = [ts_column_of(b) for b in range(B)]
+        for t in (2, 3):
+            for b in range(B):
+                gather_on_vector(w_cols[b], t, v_planes[t], entries(v_list, b))
+        u_planes.extend(load_plane(uT, t, t) for t in range(1, PACK))
 
-        h_i, h_r, w_i = {}, {}, {}
+        w_values = values_tile("values_a")
+        for u in range(2):
+            interleave(w_values, w_cols[0], u)
+        u_rounded = round_plane(u_planes[0], "u_rounded")
+        gather_on_scalar(x_cols[0], 0, u_rounded, entries(u_list, 0))
+        y_rows = []
         for b in range(B):
-            h_values = make_h(b, x_d[b], w_d[b], minus_sc[b])
-            h_i[b] = quantize(h_values, E5M2, "h_i%d" % b)
-            w_i[b] = along_list(w_cols[b], "w_i%d" % b)
-            h_r[b] = turn(lambda c, j: h_values[:, j * P : (j + 1) * P, c], E5M2, "h_r%d" % b)
-        for b in range(B):
+            y_b = held.tile([P, PACK, N], F32, name="y_rows", tag="room%d" % (4 + b), align_bytes=64)
+            for half in range(2):
+                pair = slice(2 * half, 2 * half + 2)
+                nc.sync.dma_start(y_b[:, pair, :], y[b].rearrange("(p t) i -> p t i", t=PACK)[:, pair, :])
+            y_rows.append(y_b)
+        minus_sc = scales_of(0, ts_columns[0])
+        for t in (1, 2):
+            for b in range(B):
+                gather_on_vector(x_cols[b], t, u_planes[t], entries(u_list, b))
+        gather_on_vector(x_cols[0], 3, u_planes[3], entries(u_list, 0))
+        w_d = operand(E4M3, "w_d0", "room2")
+        quantize(w_d, w_values, slice(0, K))
+        x_values = values_tile("values_b")
+        x_d = operand(E4M3, "x_d0")
+        for u in range(2):
+            quantize(x_d, x_values, interleave(x_values, x_cols[0], u))
+        gather_on_vector(x_cols[1], 3, u_planes[3], entries(u_list, 1))
+        gather_on_scalar(x_cols[1], 0, u_rounded, entries(u_list, 1))
+
+        h_values = make_h(0, x_d, w_d, minus_sc)
+        w_i = along_list(w_cols[0], "w_i0", "values_b")
+        h_i = operand(E5M2, "h_i0")
+        quantize(h_i, h_values, slice(0, K))
+        x_r = along_list(x_cols[0], "x_r0", "values_d")
+        scatter(1, 0, 0, result_of((w_i, h_i), 0, "acc0"))
+        h_r = h_along_rows(h_values, "h_r0")
+        for t in (1, 2):
+            scatter(1, t, 0, result_of((w_i, h_i), t, "acc%d" % (t % 2)))
+        first_du, first_dv = (w_i, h_i), (x_r, h_r)
+
+        w_d = along_d(w_cols[1], "w_d1", "values_a")
+        minus_sc = scales_of(1, ts_columns[1])
+        x_r = along_list(x_cols[1], "x_r1", "values_d")
+        x_d = along_d(x_cols[1], "x_d1", "values_c")
+        scatter(1, 3, 0, result_of(first_du, 3, "acc1", "x_cols1"))
+        w_i = along_list(w_cols[1], "w_i1", "values_b")
+        h_values = make_h(1, x_d, w_d, minus_sc)
+        h_i = operand(E5M2, "h_i1")
+        quantize(h_i, h_values, slice(0, K))
+        h_r = h_along_rows(h_values, "h_r1")
+        for t, bank in enumerate(("acc0", "acc1", "acc0", "gap3")):
+            scatter(0, t, 0, result_of(first_dv, t, bank))
+        for o, operands in ((1, (w_i, h_i)), (0, (x_r, h_r))):
             for t in range(PACK):
-                finish(1, t, b, w_i[b], h_i[b])
-                finish(0, t, b, x_r[b], h_r[b])
+                scatter(o, t, 1, result_of(operands, t, "acc%d" % (t % 2)))

@@ -28,7 +28,7 @@ def tile_attend_gmf_lch_vu_kernel(tc, uT, vT, y, us, ts, offs, uoffs, out_0, out
     nc = tc.nc
     with ExitStack() as ctx:
         held = ctx.enter_context(tc.tile_pool(name="held", bufs=1))
-        ring = ctx.enter_context(tc.tile_pool(name="ring", bufs=4))
+        ring = ctx.enter_context(tc.tile_pool(name="ring", bufs=3))
         staged = ctx.enter_context(tc.tile_pool(name="staged", bufs=4))
         psum = ctx.enter_context(tc.psum_pool(name="psum", bufs=1))
 
@@ -48,8 +48,9 @@ def tile_attend_gmf_lch_vu_kernel(tc, uT, vT, y, us, ts, offs, uoffs, out_0, out
         nc.vector.memset(ts_row[32:64, :], 0.0)
         nc.vector.memset(ts_row[64:P, :], 0.0)
 
+        v_planes = [load_plane(vT, 0, 1)]
         nc.sync.dma_start(v_list[:], offs)
-        v_planes = [load_plane(vT, t, 1 + t) for t in range(2)]
+        v_planes.append(load_plane(vT, 1, 2))
         nc.sync.dma_start(u_list[:], uoffs)
         us_rows = held.tile([P, B, PACK], F32, name="us_rows")
         nc.sync.dma_start(us_rows[:], us.rearrange("b (p t) o -> p b (t o)", t=PACK))
@@ -191,15 +192,20 @@ def tile_attend_gmf_lch_vu_kernel(tc, uT, vT, y, us, ts, offs, uoffs, out_0, out
             for t in range(PACK):
                 for j in range(PACK):
                     nc.tensor.matmul(gaps[t][:, j, :], lhsT=y_rows[b][:, t, j:N:PACK], rhs=ident_f32[:], start=(j == 0), stop=False, is_transpose=True)
-                a = product(x_d, t, w_d, "acc%d" % (t % 2))
+                a = product(x_d, t, w_d, ("acc0", "acc1" if b == 0 else "turn0")[t % 2])
                 minus_a = ring.tile([P, N], F32, name="minus_a")
-                nc.vector.scalar_tensor_tensor(minus_a[:], a[:], minus_us[:, b, t : t + 1], ts_spread[:], MULT, MULT)
+                if b == 0:
+                    nc.vector.scalar_tensor_tensor(minus_a[:], a[:], minus_us[:, b, t : t + 1], ts_spread[:], MULT, MULT)
+                else:
+                    a_us = ring.tile([P, N], F32, name="a_us")
+                    nc.scalar.activation(a_us[:], a[:], COPY, scale=minus_us[:, b, t : t + 1])
+                    nc.gpsimd.tensor_tensor(minus_a[:], a_us[:], ts_spread[:], MULT)
                 for j in range(PACK):
                     nc.tensor.matmul(gaps[t][:, j, :], lhsT=minus_a[:, j * P : (j + 1) * P], rhs=ident_f32[:], start=False, stop=(j == PACK - 1), is_transpose=True)
                 minus_g = ring.tile([P, P, PACK], F32, name="minus_g")
                 nc.scalar.activation(minus_g[:], gaps[t][:].rearrange("p j c -> p c j"), TANH)
                 rows = slice(t * P, (t + 1) * P)
-                nc.vector.tensor_tensor(values[:, rows, :], minus_g[:], minus_sc[:, :, rows].rearrange("p j c -> p c j"), MULT)
+                (nc.vector if b == 0 else nc.gpsimd).tensor_tensor(values[:, rows, :], minus_g[:], minus_sc[:, :, rows].rearrange("p j c -> p c j"), MULT)
             return values
 
         def result_of(operands, t, bank, room=None):
@@ -232,8 +238,8 @@ def tile_attend_gmf_lch_vu_kernel(tc, uT, vT, y, us, ts, offs, uoffs, out_0, out
         w_values = values_tile("values_a")
         for u in range(2):
             interleave(w_values, w_cols[0], u)
-        u_rounded = round_plane(u_planes[0], "u_rounded")
-        gather_on_scalar(x_cols[0], 0, u_rounded, entries(u_list, 0))
+        for b in range(B):
+            gather_on_vector(x_cols[b], 0, u_planes[0], entries(u_list, b))
         y_rows = []
         for b in range(B):
             y_b = held.tile([P, PACK, N], F32, name="y_rows", tag="room%d" % (4 + b), align_bytes=64)
@@ -253,7 +259,6 @@ def tile_attend_gmf_lch_vu_kernel(tc, uT, vT, y, us, ts, offs, uoffs, out_0, out
         for u in range(2):
             quantize(x_d, x_values, interleave(x_values, x_cols[0], u))
         gather_on_vector(x_cols[1], 3, u_planes[3], entries(u_list, 1))
-        gather_on_scalar(x_cols[1], 0, u_rounded, entries(u_list, 1))
 
         h_values = make_h(0, x_d, w_d, minus_sc)
         w_i = along_list(w_cols[0], "w_i0", "values_b")
@@ -271,13 +276,14 @@ def tile_attend_gmf_lch_vu_kernel(tc, uT, vT, y, us, ts, offs, uoffs, out_0, out
         x_r = along_list(x_cols[1], "x_r1", "values_d")
         x_d = along_d(x_cols[1], "x_d1", "values_c")
         scatter(1, 3, 0, result_of(first_du, 3, "acc1", "x_cols1"))
-        w_i = along_list(w_cols[1], "w_i1", "values_b")
+        for t in range(PACK - 1):
+            scatter(0, t, 0, result_of(first_dv, t, "acc1"))
         h_values = make_h(1, x_d, w_d, minus_sc)
+        w_i = along_list(w_cols[1], "w_i1", "values_b")
         h_i = operand(E5M2, "h_i1")
         quantize(h_i, h_values, slice(0, K))
         h_r = h_along_rows(h_values, "h_r1")
-        for t, bank in enumerate(("acc0", "acc1", "acc0", "gap3")):
-            scatter(0, t, 0, result_of(first_dv, t, bank))
+        scatter(0, PACK - 1, 0, result_of(first_dv, PACK - 1, "acc1", "minus_sc"))
         for o, operands in ((1, (w_i, h_i)), (0, (x_r, h_r))):
             for t in range(PACK):
                 scatter(o, t, 1, result_of(operands, t, "acc%d" % (t % 2)))

@@ -45,29 +45,27 @@ def tile_attend_gmf_lch_vu_kernel(tc, uT, vT, y, us, ts, offs, uoffs, out_0, out
 
         ts_row = held.tile([P, T], F32, name="ts_row", tag="room0")
         nc.scalar.dma_start(ts_row[0:32, :], ts[0:32, :])
-        nc.vector.memset(ts_row[32:64, :], 0.0)
         nc.vector.memset(ts_row[64:P, :], 0.0)
 
-        v_planes = [load_plane(vT, 0, 1)]
-        nc.sync.dma_start(v_list[:], offs)
-        v_planes.append(load_plane(vT, 1, 2))
-        nc.sync.dma_start(u_list[:], uoffs)
         us_rows = held.tile([P, B, PACK], F32, name="us_rows")
-        nc.sync.dma_start(us_rows[:], us.rearrange("b (p t) o -> p b (t o)", t=PACK))
-        v_planes.extend(load_plane(vT, t, 1 + t) for t in range(2, PACK))
+        nc.scalar.dma_start(us_rows[:], us.rearrange("b (p t) o -> p b (t o)", t=PACK))
+        nc.sync.dma_start(v_list[:], offs)
+        nc.sync.dma_start(u_list[:], uoffs)
+        v_planes = [load_plane(vT, t, 1 + t) for t in range(PACK)]
         u_planes = [load_plane(uT, 0, 5)]
 
         ident_bf = held.tile([P, P], BF16, name="ident_bf")
         ident_f32 = held.tile([P, P], F32, name="ident_f32")
         make_identity(nc, ident_f32[:])
+        nc.gpsimd.memset(ts_row[32:64, :], 0.0)
         make_identity(nc, ident_bf[:])
 
         windows = {}
-        for n, (t, o) in enumerate((t, o) for t in range(PACK) for o in (1, 0)):
+        for o, t in ((o, t) for o in (1, 0) for t in range(PACK)):
             windows[o, t] = held.tile([P, T], F32, name="window%d%d" % (o, t))
-            (nc.vector if n < 1 else nc.gpsimd).memset(windows[o, t][:], 0.0)
+            nc.gpsimd.memset(windows[o, t][:], 0.0)
 
-        x_cols = [held.tile([P, PACK, K], BF16, name="x_cols", tag="x_cols%d" % b) for b in range(B)]
+        x_cols = [held.tile([P, PACK, K], BF16, name="x_cols", tag="x_cols%d" % b, align_bytes=64) for b in range(B)]
         w_cols = [held.tile([P, PACK, K], BF16, name="w_cols%d" % b) for b in range(B)]
 
         def gathered(cols, t):
@@ -110,28 +108,30 @@ def tile_attend_gmf_lch_vu_kernel(tc, uT, vT, y, us, ts, offs, uoffs, out_0, out
         def values_tile(tag):
             return held.tile([P, K, PACK], BF16, name="values", tag=tag, align_bytes=64)
 
-        def interleave(values, cols, u):
+        def interleave(values, cols, u, on_gpsimd=False):
             half = slice(u * HALF, (u + 1) * HALF)
-            nc.scalar.copy(
-                values[:, half, :].rearrange("p (e m) t -> p e m t", e=2),
-                cols[:, :, half].rearrange("p t (m e) -> p e m t", e=2),
-            )
+            target = values[:, half, :].rearrange("p (e m) t -> p e m t", e=2)
+            source = cols[:, :, half].rearrange("p t (m e) -> p e m t", e=2)
+            if on_gpsimd:
+                nc.gpsimd.tensor_scalar(target, source, 1.0, 0.0, MULT, mybir.AluOpType.add)
+            else:
+                nc.scalar.copy(target, source)
             return half
 
-        def along_d(cols, name, tag):
+        def along_d(cols, name, tag, on_gpsimd=False):
             values = values_tile(tag)
             for u in range(2):
-                interleave(values, cols, u)
+                interleave(values, cols, u, on_gpsimd)
             target = operand(E4M3, name)
             quantize(target, values, slice(0, K))
             return target
 
-        def along_list(cols, name, tag):
+        def along_list(cols, name, tag, banks):
             values = values_tile(tag)
             pairs = cols[:].bitcast(F32)
             value_pairs = values[:].bitcast(F32)
             for half in range(2):
-                turned = psum.tile([P, 2, 2, P], F32, name="turned", tag="turn%d" % half)
+                turned = psum.tile([P, 2, 2, P], F32, name="turned", tag=banks[half])
                 for e in range(2):
                     for u in range(2):
                         nc.tensor.transpose(turned[:, e, u, :], pairs[:, 2 * half + e, u * P : (u + 1) * P], ident_f32[:])
@@ -146,7 +146,7 @@ def tile_attend_gmf_lch_vu_kernel(tc, uT, vT, y, us, ts, offs, uoffs, out_0, out
         def h_along_rows(h_values, name):
             values = values_tile("values_c")
             for half in range(2):
-                turned = psum.tile([P, 2, PACK, P], BF16, name="turned", tag="turn%d" % half)
+                turned = psum.tile([P, 2, PACK, P], BF16, name="turned", tag="acc%d" % half)
                 for e in range(2):
                     for t in range(PACK):
                         nc.tensor.transpose(turned[:, e, t, :], h_values[:, t * P : (t + 1) * P, 2 * half + e], ident_bf[:])
@@ -180,7 +180,7 @@ def tile_attend_gmf_lch_vu_kernel(tc, uT, vT, y, us, ts, offs, uoffs, out_0, out
             ts_spread = held.tile([P, N], F32, name="ts_spread")
             nc.scalar.copy(ts_spread[:], spread(ts_column, "gap2"))
             us_spread = spread(minus_us[:, b, :], "gap3")
-            minus_sc = held.tile([P, PACK, R], F32, name="minus_sc")
+            minus_sc = held.tile([P, PACK, R], F32, name="minus_sc", align_bytes=64)
             for j in range(PACK):
                 nc.scalar.activation(minus_sc[:, j, :], us_spread, COPY, scale=ts_column[:, j : j + 1])
             return ts_spread, minus_sc
@@ -191,7 +191,7 @@ def tile_attend_gmf_lch_vu_kernel(tc, uT, vT, y, us, ts, offs, uoffs, out_0, out
             gaps = [psum.tile([P, PACK, P], F32, name="gap", tag="gap%d" % t) for t in range(PACK)]
             for t in range(PACK):
                 for j in range(PACK):
-                    nc.tensor.matmul(gaps[t][:, j, :], lhsT=y_rows[b][:, t, j:N:PACK], rhs=ident_f32[:], start=(j == 0), stop=False, is_transpose=True)
+                    nc.tensor.matmul(gaps[t][:, j, :], lhsT=y_rows[b, t][:, j:N:PACK], rhs=ident_f32[:], start=(j == 0), stop=False, is_transpose=True)
                 a = product(x_d, t, w_d, ("acc0", "acc1" if b == 0 else "turn0")[t % 2])
                 minus_a = ring.tile([P, N], F32, name="minus_a")
                 if b == 0:
@@ -213,7 +213,7 @@ def tile_attend_gmf_lch_vu_kernel(tc, uT, vT, y, us, ts, offs, uoffs, out_0, out
             if room is None:
                 result = staged.tile([P, P, PACK], F32, name="result")
             else:
-                result = held.tile([P, P, PACK], F32, name="result", tag=room)
+                result = held.tile([P, P, PACK], F32, name="result", tag=room, align_bytes=64)
             nc.scalar.copy(result[:], acc[:].rearrange("p (j m) -> p m j", j=PACK))
             return result
 
@@ -233,24 +233,29 @@ def tile_attend_gmf_lch_vu_kernel(tc, uT, vT, y, us, ts, offs, uoffs, out_0, out
         for t in (2, 3):
             for b in range(B):
                 gather_on_vector(w_cols[b], t, v_planes[t], entries(v_list, b))
-        u_planes.extend(load_plane(uT, t, t) for t in range(1, PACK))
+        u_planes.extend(load_plane(uT, t, t) for t in (1, 2))
+
+        def load_y(b, tiles, room):
+            y_part = held.tile([P, len(tiles), N], F32, name="y_part", tag="room%d" % room, align_bytes=64)
+            nc.sync.dma_start(y_part[:], y[b].rearrange("(p t) i -> p t i", t=PACK)[:, tiles.start : tiles.stop, :])
+            for t in tiles:
+                y_rows[b, t] = y_part[:, t - tiles.start, :]
+
+        y_rows = {}
+        load_y(0, range(0, 2), 3)
+        u_planes.append(load_plane(uT, 3, 4))
 
         w_values = values_tile("values_a")
         for u in range(2):
             interleave(w_values, w_cols[0], u)
         for b in range(B):
             gather_on_vector(x_cols[b], 0, u_planes[0], entries(u_list, b))
-        y_rows = []
-        for b in range(B):
-            y_b = held.tile([P, PACK, N], F32, name="y_rows", tag="room%d" % (4 + b), align_bytes=64)
-            for half in range(2):
-                pair = slice(2 * half, 2 * half + 2)
-                nc.sync.dma_start(y_b[:, pair, :], y[b].rearrange("(p t) i -> p t i", t=PACK)[:, pair, :])
-            y_rows.append(y_b)
+        load_y(0, range(2, PACK), 5)
         minus_sc = scales_of(0, ts_columns[0])
         for t in (1, 2):
             for b in range(B):
                 gather_on_vector(x_cols[b], t, u_planes[t], entries(u_list, b))
+        load_y(1, range(PACK), 1)
         gather_on_vector(x_cols[0], 3, u_planes[3], entries(u_list, 0))
         w_d = operand(E4M3, "w_d0", "room2")
         quantize(w_d, w_values, slice(0, K))
@@ -261,29 +266,33 @@ def tile_attend_gmf_lch_vu_kernel(tc, uT, vT, y, us, ts, offs, uoffs, out_0, out
         gather_on_vector(x_cols[1], 3, u_planes[3], entries(u_list, 1))
 
         h_values = make_h(0, x_d, w_d, minus_sc)
-        w_i = along_list(w_cols[0], "w_i0", "values_b")
+        w_i = along_list(w_cols[0], "w_i0", "values_b", ("turn0", "turn1"))
         h_i = operand(E5M2, "h_i0")
         quantize(h_i, h_values, slice(0, K))
-        x_r = along_list(x_cols[0], "x_r0", "values_d")
-        scatter(1, 0, 0, result_of((w_i, h_i), 0, "acc0"))
+        first_du = (w_i, h_i)
+        scatter(1, 0, 0, result_of(first_du, 0, "acc0", "first_result"))
+        scatter(1, 1, 0, result_of(first_du, 1, "acc1"))
         h_r = h_along_rows(h_values, "h_r0")
-        for t in (1, 2):
-            scatter(1, t, 0, result_of((w_i, h_i), t, "acc%d" % (t % 2)))
-        first_du, first_dv = (w_i, h_i), (x_r, h_r)
+        x_r = along_list(x_cols[0], "x_r0", "values_d", ("gap2", "gap3"))
+        scatter(1, 2, 0, result_of(first_du, 2, "acc0"))
+        first_dv = (x_r, h_r)
 
-        w_d = along_d(w_cols[1], "w_d1", "values_a")
+        w_d = along_d(w_cols[1], "w_d1", "first_result", True)
         minus_sc = scales_of(1, ts_columns[1])
-        x_r = along_list(x_cols[1], "x_r1", "values_d")
-        x_d = along_d(x_cols[1], "x_d1", "values_c")
+        x_r = along_list(x_cols[1], "x_r1", "values_d", ("turn0", "turn1"))
+        x_d = along_d(x_cols[1], "x_d1", "values_a")
         scatter(1, 3, 0, result_of(first_du, 3, "acc1", "x_cols1"))
         for t in range(PACK - 1):
             scatter(0, t, 0, result_of(first_dv, t, "acc1"))
         h_values = make_h(1, x_d, w_d, minus_sc)
-        w_i = along_list(w_cols[1], "w_i1", "values_b")
+        w_i = along_list(w_cols[1], "w_i1", "values_b", ("turn0", "turn1"))
         h_i = operand(E5M2, "h_i1")
         quantize(h_i, h_values, slice(0, K))
-        h_r = h_along_rows(h_values, "h_r1")
         scatter(0, PACK - 1, 0, result_of(first_dv, PACK - 1, "acc1", "minus_sc"))
-        for o, operands in ((1, (w_i, h_i)), (0, (x_r, h_r))):
-            for t in range(PACK):
-                scatter(o, t, 1, result_of(operands, t, "acc%d" % (t % 2)))
+        for t in range(2):
+            scatter(1, t, 1, result_of((w_i, h_i), t, "acc%d" % t))
+        h_r = h_along_rows(h_values, "h_r1")
+        for t in range(2, PACK):
+            scatter(1, t, 1, result_of((w_i, h_i), t, "turn%d" % (t % 2)))
+        for t in range(PACK):
+            scatter(0, t, 1, result_of((x_r, h_r), t, "acc%d" % (t % 2)))

from contextlib import ExitStack

import concourse.mybir as mybir
from concourse.masks import make_identity

B, N, T, D, R, TU = 2, 512, 2048, 512, 512, 2048
FLOPS = 3 * 2 * B * R * N * D

F32 = mybir.dt.float32
BF16 = mybir.dt.bfloat16
U32 = mybir.dt.uint32
U16 = mybir.dt.uint16
U8 = mybir.dt.uint8
E4M3 = mybir.dt.float8_e4m3fn_x4
E5M2 = mybir.dt.float8_e5m2_x4
COPY = mybir.ActivationFunctionType.Copy
TANH = mybir.ActivationFunctionType.Tanh
MULT = mybir.AluOpType.mult

P = 128
PACK = 4
K = P * PACK
HALF = K // 2
LIST_COLS = K // 16


def tile_attend_gmf_lch_vu_kernel(tc, uT, vT, y, us, ts, offs, uoffs, out_0, out_1):
    nc = tc.nc
    with ExitStack() as ctx:
        held = ctx.enter_context(tc.tile_pool(name="held", bufs=1))
        ring = ctx.enter_context(tc.tile_pool(name="ring", bufs=3))
        staged = ctx.enter_context(tc.tile_pool(name="staged", bufs=4))
        psum = ctx.enter_context(tc.psum_pool(name="psum", bufs=1))

        u_list = held.tile([P, B * LIST_COLS], U16, name="u_list")
        v_list = held.tile([P, B * LIST_COLS], U16, name="v_list")

        def entries(a_list, b):
            return a_list[:, b * LIST_COLS : (b + 1) * LIST_COLS]

        def load_plane(table, t, room):
            plane = held.tile([P, T], F32, name="plane", tag="room%d" % room, align_bytes=64)
            nc.sync.dma_start(plane[:], table.rearrange("(p t) c -> p t c", t=PACK)[:, t, :])
            return plane

        ts_row = held.tile([P, T], F32, name="ts_row", tag="room0")
        nc.scalar.dma_start(ts_row[0:32, :], ts[0:32, :])
        nc.vector.memset(ts_row[64:P, :], 0.0)

        us_rows = held.tile([P, B, PACK], F32, name="us_rows")
        nc.scalar.dma_start(us_rows[:], us.rearrange("b (p t) o -> p b (t o)", t=PACK))
        nc.sync.dma_start(v_list[:], offs)
        nc.sync.dma_start(u_list[:], uoffs)
        v_planes = [load_plane(vT, t, 1 + t) for t in range(PACK)]
        u_planes = [load_plane(uT, 0, 5)]

        ident_bf = held.tile([P, P], BF16, name="ident_bf")
        ident_f32 = held.tile([P, P], F32, name="ident_f32")
        make_identity(nc, ident_f32[:])
        nc.gpsimd.memset(ts_row[32:64, :], 0.0)
        make_identity(nc, ident_bf[:])

        windows = {}
        for o, t in ((o, t) for o in (1, 0) for t in range(PACK)):
            windows[o, t] = held.tile([P, T], F32, name="window%d%d" % (o, t))
            nc.gpsimd.memset(windows[o, t][:], 0.0)

        x_cols = [held.tile([P, PACK, K], BF16, name="x_cols", tag="x_cols%d" % b, align_bytes=64) for b in range(B)]
        w_cols = [held.tile([P, PACK, K], BF16, name="w_cols%d" % b) for b in range(B)]

        def gathered(cols, t):
            return cols[:, t, :].rearrange("p (u m e) -> p m u e", u=2, e=2)

        def gather_on_vector(cols, t, plane, offsets):
            nc.vector.tensor_copy(gathered(cols, t), plane[:].indirect(offsets))

        def gather_on_scalar(cols, t, rounded, offsets):
            nc.scalar.activation(gathered(cols, t), rounded[:].indirect(offsets), COPY)

        def round_plane(plane, name):
            rounded = held.tile([P, T], BF16, name=name)
            nc.scalar.activation(rounded[:], plane[:], COPY)
            return rounded

        def operand(fmt, name, room=None):
            codes = held.tile([P, K], U32, name=name + "_codes", tag=room or name + "_codes", align_bytes=64)
            scales = held.tile([P, K], U8, name=name + "_scales", align_bytes=64)
            return codes, scales, fmt

        def quantize(target, values, cols):
            codes, scales, fmt = target
            nc.vector.quantize_mx(out=codes[:, cols].bitcast(fmt), scales=scales[:, cols], in_=values[:, cols, :].rearrange("p c t -> p (c t)"))

        def product(stationary, j, moving, bank):
            acc = psum.tile([P, K], F32, name="acc", tag=bank)
            cols = slice(j * P, (j + 1) * P)
            nc.tensor.matmul_mx(
                out=acc[:],
                lhsT=stationary[0][:, cols].bitcast(stationary[2]),
                lhsT_scale=stationary[1][:, cols],
                rhs=moving[0][:].bitcast(moving[2]),
                rhs_scale=moving[1][:],
                start=True,
                stop=True,
            )
            return acc

        def values_tile(tag):
            return held.tile([P, K, PACK], BF16, name="values", tag=tag, align_bytes=64)

        def interleave(values, cols, u, on_gpsimd=False):
            half = slice(u * HALF, (u + 1) * HALF)
            target = values[:, half, :].rearrange("p (e m) t -> p e m t", e=2)
            source = cols[:, :, half].rearrange("p t (m e) -> p e m t", e=2)
            if on_gpsimd:
                nc.gpsimd.tensor_scalar(target, source, 1.0, 0.0, MULT, mybir.AluOpType.add)
            else:
                nc.scalar.copy(target, source)
            return half

        def along_d(cols, name, tag, on_gpsimd=False):
            values = values_tile(tag)
            for u in range(2):
                interleave(values, cols, u, on_gpsimd)
            target = operand(E4M3, name)
            quantize(target, values, slice(0, K))
            return target

        def along_list(cols, name, tag, banks):
            values = values_tile(tag)
            pairs = cols[:].bitcast(F32)
            value_pairs = values[:].bitcast(F32)
            for half in range(2):
                turned = psum.tile([P, 2, 2, P], F32, name="turned", tag=banks[half])
                for e in range(2):
                    for u in range(2):
                        nc.tensor.transpose(turned[:, e, u, :], pairs[:, 2 * half + e, u * P : (u + 1) * P], ident_f32[:])
                nc.scalar.copy(
                    value_pairs[:, half * HALF : (half + 1) * HALF, :].rearrange("p (e c) u -> p e c u", e=2),
                    turned[:].rearrange("p e u c -> p e c u"),
                )
            target = operand(E4M3, name)
            quantize(target, values, slice(0, K))
            return target

        def h_along_rows(h_values, name):
            values = values_tile("values_c")
            for half in range(2):
                turned = psum.tile([P, 2, PACK, P], BF16, name="turned", tag="acc%d" % half)
                for e in range(2):
                    for t in range(PACK):
                        nc.tensor.transpose(turned[:, e, t, :], h_values[:, t * P : (t + 1) * P, 2 * half + e], ident_bf[:])
                nc.scalar.copy(
                    values[:, half * HALF : (half + 1) * HALF, :].rearrange("p (e m) t -> p e m t", e=2),
                    turned[:].rearrange("p e t m -> p e m t"),
                )
            target = operand(E5M2, name)
            quantize(target, values, slice(0, K))
            return target

        minus_us = held.tile([P, B, PACK], F32, name="minus_us")

        def ts_column_of(b):
            ts_slots = held.tile([P, N], F32, name="ts_slots%d" % b)
            nc.vector.tensor_copy(ts_slots[:], ts_row[:].indirect(entries(v_list, b)))
            turned = psum.tile([P, PACK, P], F32, name="turned", tag="gap%d" % b)
            for j in range(PACK):
                nc.tensor.transpose(turned[:, j, :], ts_slots[:, j:N:PACK], ident_f32[:])
            ts_column = held.tile([P, PACK], F32, name="ts_column%d" % b)
            nc.scalar.copy(ts_column[:], turned[:, :, 0])
            return ts_column

        def spread(columns, bank):
            rows = psum.tile([P, PACK, P], F32, name="rows", tag=bank)
            for j in range(PACK):
                nc.tensor.transpose(rows[:, j, :], columns[:, j : j + 1].to_broadcast([P, P]), ident_f32[:])
            return rows[:].rearrange("p j m -> p (j m)")

        def scales_of(b, ts_column):
            ts_spread = held.tile([P, N], F32, name="ts_spread")
            nc.scalar.copy(ts_spread[:], spread(ts_column, "gap2"))
            us_spread = spread(minus_us[:, b, :], "gap3")
            minus_sc = held.tile([P, PACK, R], F32, name="minus_sc", align_bytes=64)
            for j in range(PACK):
                nc.scalar.activation(minus_sc[:, j, :], us_spread, COPY, scale=ts_column[:, j : j + 1])
            return ts_spread, minus_sc

        def make_h(b, x_d, w_d, scales):
            ts_spread, minus_sc = scales
            values = values_tile("values_a")
            gaps = [psum.tile([P, PACK, P], F32, name="gap", tag="gap%d" % t) for t in range(PACK)]
            for t in range(PACK):
                for j in range(PACK):
                    nc.tensor.matmul(gaps[t][:, j, :], lhsT=y_rows[b, t][:, j:N:PACK], rhs=ident_f32[:], start=(j == 0), stop=False, is_transpose=True)
                a = product(x_d, t, w_d, ("acc0", "acc1" if b == 0 else "turn0")[t % 2])
                minus_a = ring.tile([P, N], F32, name="minus_a")
                if b == 0:
                    nc.vector.scalar_tensor_tensor(minus_a[:], a[:], minus_us[:, b, t : t + 1], ts_spread[:], MULT, MULT)
                else:
                    a_us = ring.tile([P, N], F32, name="a_us")
                    nc.scalar.activation(a_us[:], a[:], COPY, scale=minus_us[:, b, t : t + 1])
                    nc.gpsimd.tensor_tensor(minus_a[:], a_us[:], ts_spread[:], MULT)
                for j in range(PACK):
                    nc.tensor.matmul(gaps[t][:, j, :], lhsT=minus_a[:, j * P : (j + 1) * P], rhs=ident_f32[:], start=False, stop=(j == PACK - 1), is_transpose=True)
                minus_g = ring.tile([P, P, PACK], F32, name="minus_g")
                nc.scalar.activation(minus_g[:], gaps[t][:].rearrange("p j c -> p c j"), TANH)
                rows = slice(t * P, (t + 1) * P)
                (nc.vector if b == 0 else nc.gpsimd).tensor_tensor(values[:, rows, :], minus_g[:], minus_sc[:, :, rows].rearrange("p j c -> p c j"), MULT)
            return values

        def result_of(operands, t, bank, room=None):
            acc = product(operands[0], t, operands[1], bank)
            if room is None:
                result = staged.tile([P, P, PACK], F32, name="result")
            else:
                result = held.tile([P, P, PACK], F32, name="result", tag=room, align_bytes=64)
            nc.scalar.copy(result[:], acc[:].rearrange("p (j m) -> p m j", j=PACK))
            return result

        def scatter(o, t, b, result):
            a_list = (v_list, u_list)[o]
            nc.vector.tensor_copy(windows[o, t][:].indirect(entries(a_list, b)), result[:].rearrange("p m j -> p (m j)"))
            if b == B - 1:
                nc.sync.dma_start((out_0, out_1)[o].rearrange("(p t) c -> p t c", t=PACK)[:, t, :], windows[o, t][:])

        for b in range(B):
            gather_on_vector(w_cols[b], 0, v_planes[0], entries(v_list, b))
        v_rounded = round_plane(v_planes[1], "v_rounded")
        for b in range(B):
            gather_on_scalar(w_cols[b], 1, v_rounded, entries(v_list, b))
        nc.vector.tensor_scalar_mul(minus_us[:], us_rows[:], -1.0)
        ts_columns = [ts_column_of(b) for b in range(B)]
        for t in (2, 3):
            for b in range(B):
                gather_on_vector(w_cols[b], t, v_planes[t], entries(v_list, b))
        u_planes.extend(load_plane(uT, t, t) for t in (1, 2))

        def load_y(b, tiles, room):
            y_part = held.tile([P, len(tiles), N], F32, name="y_part", tag="room%d" % room, align_bytes=64)
            nc.sync.dma_start(y_part[:], y[b].rearrange("(p t) i -> p t i", t=PACK)[:, tiles.start : tiles.stop, :])
            for t in tiles:
                y_rows[b, t] = y_part[:, t - tiles.start, :]

        y_rows = {}
        load_y(0, range(0, 2), 3)
        u_planes.append(load_plane(uT, 3, 4))

        w_values = values_tile("values_a")
        for u in range(2):
            interleave(w_values, w_cols[0], u)
        for b in range(B):
            gather_on_vector(x_cols[b], 0, u_planes[0], entries(u_list, b))
        load_y(0, range(2, PACK), 5)
        minus_sc = scales_of(0, ts_columns[0])
        for t in (1, 2):
            for b in range(B):
                gather_on_vector(x_cols[b], t, u_planes[t], entries(u_list, b))
        load_y(1, range(PACK), 1)
        gather_on_vector(x_cols[0], 3, u_planes[3], entries(u_list, 0))
        w_d = operand(E4M3, "w_d0", "room2")
        quantize(w_d, w_values, slice(0, K))
        x_values = values_tile("values_b")
        x_d = operand(E4M3, "x_d0")
        for u in range(2):
            quantize(x_d, x_values, interleave(x_values, x_cols[0], u))
        gather_on_vector(x_cols[1], 3, u_planes[3], entries(u_list, 1))

        h_values = make_h(0, x_d, w_d, minus_sc)
        w_i = along_list(w_cols[0], "w_i0", "values_b", ("turn0", "turn1"))
        h_i = operand(E5M2, "h_i0")
        quantize(h_i, h_values, slice(0, K))
        first_du = (w_i, h_i)
        scatter(1, 0, 0, result_of(first_du, 0, "acc0", "first_result"))
        scatter(1, 1, 0, result_of(first_du, 1, "acc1"))
        h_r = h_along_rows(h_values, "h_r0")
        x_r = along_list(x_cols[0], "x_r0", "values_d", ("gap2", "gap3"))
        scatter(1, 2, 0, result_of(first_du, 2, "acc0"))
        first_dv = (x_r, h_r)

        w_d = along_d(w_cols[1], "w_d1", "first_result", True)
        minus_sc = scales_of(1, ts_columns[1])
        x_r = along_list(x_cols[1], "x_r1", "values_d", ("turn0", "turn1"))
        x_d = along_d(x_cols[1], "x_d1", "values_a")
        scatter(1, 3, 0, result_of(first_du, 3, "acc1", "x_cols1"))
        for t in range(PACK - 1):
            scatter(0, t, 0, result_of(first_dv, t, "acc1"))
        h_values = make_h(1, x_d, w_d, minus_sc)
        w_i = along_list(w_cols[1], "w_i1", "values_b", ("turn0", "turn1"))
        h_i = operand(E5M2, "h_i1")
        quantize(h_i, h_values, slice(0, K))
        scatter(0, PACK - 1, 0, result_of(first_dv, PACK - 1, "acc1", "minus_sc"))
        for t in range(2):
            scatter(1, t, 1, result_of((w_i, h_i), t, "acc%d" % t))
        h_r = h_along_rows(h_values, "h_r1")
        for t in range(2, PACK):
            scatter(1, t, 1, result_of((w_i, h_i), t, "turn%d" % (t % 2)))
        for t in range(PACK):
            scatter(0, t, 1, result_of((x_r, h_r), t, "acc%d" % (t % 2)))
